import numpy as np, ml_dtypes
CORES = [2,3,42,43,82,83,122,123]
N = 8
BF = ml_dtypes.bfloat16
W, RO, F, INV = 3072, 4, 1, 1
def rises(g):
    return np.sum(g > np.arange(W), axis=-1)
def perms(rng, *shape):
    return np.argsort(rng.random(shape + (W,)), axis=-1)
def some(rng, m):
    a = np.arange(W); s = rng.permutation(W)[:m]; a[s] = rng.permutation(s)
    return a
def turned(p):
    return W - 1 - np.argsort(p)[::-1]
def lower(rng, p):
    a = np.arange(W); b = np.argsort(p); v = int(rng.choice(np.flatnonzero((p > a) & (b < a))))
    q = p.copy(); q[b[v]] = p[v]; q[v] = v
    return q
def pack(g):
    return {"g0": np.ascontiguousarray(g.reshape(N, 128, W)).astype(np.int32)}
def setup_inputs(rng):
    g = perms(rng, N, 8, 16); part = rng.random((N, 8, 16)) < 0.4
    for q, k, i in np.argwhere(part):
        g[q, k, i] = some(rng, int(W * (0.3 + 0.7 * rng.random())))
    return pack(g)
def setup_inputs_ties(rng):
    g = perms(rng, N, 8, 16)
    for k in range(4):
        b = int(rng.integers(1, 9)); o = rng.permutation(W); pr = o[:2 * b].reshape(b, 2); rings = [np.sort(x) for x in np.array_split(o[2 * b:], b)]
        for q in range(N):
            top = int(rng.integers(0, 16))
            for i in range(16):
                if i != top and rng.random() < 0.2: continue
                a = np.arange(W); swap = i == top or rng.random() < 0.5
                for s in rings: a[s] = np.roll(s, -1 if i == top else -int(rng.integers(2, 61)))
                if swap: a[pr[:, 0]] = pr[:, 1]; a[pr[:, 1]] = pr[:, 0]
                g[q, k, i] = a
    for k in range(4, 8):
        for q in range(N):
            j = int(np.argmax(rises(g[q, k]))); i = (j + int(rng.integers(1, 16))) % 16
            g[q, k, i] = turned(g[q, k, j])
    return pack(g)
def setup_inputs_ends(rng):
    a = np.arange(W); x = a.copy(); x[0] = W - 1; x[W - 1] = 0
    kinds = np.stack([a, a[::-1], np.roll(a, -1), np.roll(a, 1), x]); p = perms(rng, N, 8, 16)
    g = np.where((rng.random((N, 8, 16)) < 0.4)[..., None], p, kinds[rng.integers(0, 5, (N, 8, 16))])
    o = rng.permutation(8)
    g[:, o[0]] = a
    g[:, o[1]] = p[:, o[1]]; g[rng.integers(0, N), o[1]] = a
    g[:, o[2]] = p[:, o[2]]; g[::2, o[2], 15] = kinds[2]; g[1::2, o[2], 0] = kinds[2]
    g[:, o[3]] = p[:, o[3]]
    for q in range(N):
        m = g[q, o[3]].copy(); j = int(np.argmax(rises(m)))
        if q % 2 == 0:
            m[[j, 15]] = m[[15, j]]; c = int(rises(m[15])); m[0] = lower(rng, turned(m[15]))
            for i in range(1, 15):
                if int(rises(m[i])) == c: m[i] = lower(rng, m[i])
        else:
            m[[0, j]] = m[[j, 0]]; u = int(np.argmax(m[0])); w = int(m[0, W - 2]); m[0, u] = w; m[0, W - 2] = W - 1
            m[1] = turned(m[0]); y = m[1].copy()
            s = np.flatnonzero((a < W // 2) & (y >= W // 2)); y[s] = y[rng.permutation(s)]
            m[int(rng.integers(2, 16))] = y
        g[q, o[3]] = m
    return pack(g)
def setup_inputs_grow(rng):
    g = np.zeros((N, 8, 16, W), np.int64); m = np.exp2(1 + (np.log2(W) - 3) * rng.random((N, 8, 16))).astype(np.int64)
    for q, k, i in np.ndindex(N, 8, 16): g[q, k, i] = some(rng, int(m[q, k, i]))
    return pack(g)
def setup_inputs_alike(rng):
    p = perms(rng, N, 8, 3); p[:, :3] = p[0, :3].copy(); p[:, :, 2] = np.argsort(p[:, :, 1], axis=-1)
    g = np.take_along_axis(p, rng.integers(0, 3, (N, 8, 16))[..., None], 2)
    g[:, 7] = g[:, 7, :1].copy()
    h = W // 2 - 1
    for q in range(N):
        o = rng.permutation(W); s = np.sort(o[:h]); z = np.sort(o[h:2 * h])
        a = np.arange(W); a[s] = np.roll(s, -1); a[z] = np.roll(z, 1); b = some(rng, W // 8)
        k = rng.integers(0, 3, 16); k[rng.integers(0, 16)] = 0
        g[q, 5] = np.stack([a, b, np.argsort(b)])[k]
    o = 1 + rng.permutation(W - 3); m = W // 2
    up = np.sort(np.append(o[:m - 2], [0, W - 2])); down = np.sort(np.append(o[m - 2:], [W - 1]))[::-1]; nxt = np.roll(down, -1)
    one = np.zeros(W, np.int64); one[up] = down; one[down] = up
    two = np.zeros(W, np.int64); two[up] = nxt; two[nxt] = up
    r = int(rng.integers(0, N)); g[:, 6] = np.roll(np.arange(W), -1); g[r, 6] = one; g[(r + 1 + F) % N, 6] = two
    return pack(g)
def setup_inputs_spread(rng):
    g = np.zeros((N, 8, 16, W), np.int64)
    for q, k, i in np.ndindex(N, 8, 16):
        m = max(2, min(W, int(np.exp2(1 + (np.log2(W) - 1) * rng.random()) + 0.5)))
        if rng.random() < 0.5:
            s = np.sort(rng.permutation(W)[:m]); u = rng.random(); a = np.arange(W); a[s] = np.roll(s, -min(m - 1, 1 + int((m - 1) * u * u * u))); g[q, k, i] = a
        else: g[q, k, i] = some(rng, m)
    return pack(g)
def check_inputs(d):
    a = np.asarray(d["g0"])
    if a.shape != (N, 128, W) or np.any(np.sort(a, axis=-1) != np.arange(W)): return ["rows of g0 are permutations"]
    return []
def reference(g0):
    g = g0.astype(np.int64).reshape(N, 8, 16, W); e = rises(g)
    for t in range(RO):
        J = np.argmax(e, axis=2)
        L = np.take_along_axis(g, J[:, :, None, None], 2)
        for s in range(F + 1):
            if s == 0: M = L
            else: M = L[np.array([(r + 1 + (t * F + s - 1) % (N - 1)) % N for r in range(N)])]
            ix = np.broadcast_to(M, g.shape)
            if s > 0 and INV:
                h = np.zeros_like(g); np.put_along_axis(h, ix, g, 3)
            else: h = np.take_along_axis(g, ix, 3)
            eh = rises(h); up = eh > e
            g = np.where(up[..., None], h, g); e = np.where(up, eh, e)
    return {"yg": g.reshape(N, 128, W).astype(np.float32), "ye": e.reshape(N, 128, 1).astype(np.float32)}

import numpy as np
from concourse.mybir import AluOpType, AxisListType, ActivationFunctionType

W = 3072
RO = 4
NB = 512
CS, MID = 0.025, 1536.0
WLT = 1.0 - 2.0 ** -8
MAGIC = 12582912.0
BIG = 65536.0
HUGE = 2.0 ** 60
LOADS = [512, 512, 512, 512, 512, 256, 256]
EARLY = 3
GATH = [(384, "S"), (640, "V"), (256, "S"), (512, "V"), (480, "V"), (384, "V"), (256, "V"), (160, "V")]
CNT0 = [384, 512, 384, 512, 480, 384, 256, 160]
FIRST = 256
SEL = [512, 512, 512, 512, 512, 256]
SCAT = [512, 1280, 1024]
MIX = [(512, 0, "V"), (512, 1, "V"), (512, 3, "S"), (512, 4, "S"), (256, 7, "V"), (512, 2, "V"), (256, 5, "S")]
OUT = [(256, 0, "V"), (384, 1, "V"), (512, 2, "V"), (512, 3, "S"), (512, 4, "S"), (512, 5, "S"), (384, 7, "S")]
OWN = 128

SCRATCH = {"ps": ("psum", [128, 8 * NB], "float32")}
for _d, _list in (
        ("int32", [("Pi", W)]),
        ("float32", [("Pf", W), ("junkf", 16), ("iotaT", NB), ("Gf", 128), ("R", 128), ("st", 160), ("tc", 4), ("yec", 1),
                     ("ly", 192), ("my", 192 - OWN)]),
        ("float16", [("Ph", W), ("negselh", 768), ("iotah", NB), ("identh", 128), ("Ah", 144)]),
        ("bfloat16", [("P", W), ("P1", W), ("H0", W), ("H1", W), ("junk", W), ("junk2", 128), ("tA", FIRST), ("tB", FIRST),
                      ("neg1", 2048), ("E16", 2048), ("ones", 144), ("huge", NB), ("negsel", 768), ("codeT", NB),
                      ("ident", 128), ("nident", 128), ("wI", 128), ("Ws", 128), ("G1", 144), ("G2", 144), ("A0", 144),
                      ("A0p", 144), ("A0n", 144), ("A1", 144), ("A", 144), ("Wa", 128), ("Wna", 128), ("Wb", 128), ("Wnb", 128)]
         + [("lc%d" % _t, 192) for _t in range(RO)] + [("mc%d" % _t, 192) for _t in range(RO)]),
        ("uint16", [("mx", 192 - OWN)] + [("li%d" % _t, 192) for _t in range(RO)] + [("mi%d" % _t, 192) for _t in range(RO)])):
    for _n, _c in _list:
        SCRATCH[_n] = ("sbuf", [128, _c], _d)

SEMAPHORES = (["qV", "qS", "qT", "qG", "stored", "sent"] + ["ld%d" % k for k in range(len(LOADS))]
              + ["ah%d" % t for t in range(RO)] + ["ai%d" % t for t in range(RO)] + ["ac%d" % t for t in range(RO)])


def spans(sizes, a=0):
    out = []
    for n in sizes:
        out.append((a, a + n))
        a += n
    return out


def emit(g, T, ops):
    queue = {"V": g.vector, "S": g.scalar, "T": g.tensor, "G": g, "Y": g.sync}
    seen = {}
    deps = []
    for n, op in enumerate(ops):
        last, other = {}, set()
        acc = [(b, lo, hi, False) for b, lo, hi in op["r"]] + [(b, lo, hi, True) for b, lo, hi in op["w"]]
        acc = [(b, lo // NB * NB, -(-hi // NB) * NB, wr) if b == "ps" else (b, lo, hi, wr) for b, lo, hi, wr in acc]
        for b, lo, hi, wr in acc:
            for m, l2, h2, w2 in seen.get(b, []):
                if l2 >= hi or lo >= h2:
                    continue
                p = ops[m]
                if p["sem"] is not None:
                    if wr or w2:
                        other.add(m)
                    continue
                need = p["q"] != op["q"] if b == "ps" else (wr or w2)
                if need:
                    last[p["q"]] = max(last.get(p["q"], -1), m)
        for b, lo, hi, wr in acc:
            seen.setdefault(b, []).append((n, lo, hi, wr))
        deps.append((last, other))
    know = {q: {} for q in queue}
    after = []
    waits = []
    for n, op in enumerate(ops):
        k = know[op["q"]]
        last, other = deps[n]
        ws = []
        for m in sorted(list(last.values()) + list(other), reverse=True):
            key = ops[m]["q"] if ops[m]["sem"] is None else ("x", m)
            if k.get(key, -1) >= m:
                continue
            ws.append(m)
            for kk, v in after[m].items():
                if k.get(kk, -1) < v:
                    k[kk] = v
        waits.append(ws)
        a = dict(k)
        a[op["q"] if op["sem"] is None else ("x", n)] = n
        after.append(a)
    marked = set()
    for ws in waits:
        marked.update(ws)
    count = {q: 0 for q in queue}
    value = {}
    for n, op in enumerate(ops):
        q = queue[op["q"]]
        for m in waits[n]:
            s, v = value[m]
            q.wait_ge(T.sem[s], v)
        if op["sem"] is not None:
            value[n] = op["sem"]
            if op["f"] is not None:
                op["f"]()
            continue
        ins = op["f"]()
        if n in marked:
            count[op["q"]] += 1
            value[n] = ("q" + op["q"], count[op["q"]])
            ins.then_inc(T.sem["q" + op["q"]], 1)


def rank_program(g, core, T, topo):
    rank = T.rank_of(core)
    if rank is None:
        return
    cores = list(T.cores)
    n_ranks = len(cores)
    dests = [cores[(rank - 1 - t % (n_ranks - 1)) % n_ranks] for t in range(RO)]
    srcs = [cores[(rank + 1 + t % (n_ranks - 1)) % n_ranks] for t in range(RO)]

    def engines_of(c):
        r = cores.index(c)
        ds = [cores[(r - 1 - t % (n_ranks - 1)) % n_ranks] for t in range(RO)]
        return [e for e in topo.engines(c, ds[0]) if all(e in topo.engines(c, d) for d in ds)]

    my_eng = engines_of(core)
    my_mask = sum(1 << e for e in my_eng)

    AF, ALU = ActivationFunctionType, AluOpType
    V, S, PE = g.vector, g.scalar, g.tensor
    ops = []

    def op(q, f, r=(), w=(), sem=None):
        ops.append({"q": q, "f": f, "r": list(r), "w": list(w), "sem": sem})

    def col(j):
        return T.st[:, j:j + 1]

    def rc(j, n=1):
        return ("st", j, j + n)

    def al(name):
        return (name, 0, SCRATCH[name][1][1])

    def act(out, in_, func, r, w, **kw):
        op("S", lambda: S.activation(out, in_, func, **kw), r, w)

    def ts(out, in0, s1, s2, o0, o1, r, w):
        if o1 is None:
            op("V", lambda: V.tensor_scalar(out, in0, s1, None, o0), r, w)
        else:
            op("V", lambda: V.tensor_scalar(out, in0, s1, s2, o0, o1), r, w)

    def vcopy(out, in_, r, w):
        op("V", lambda: V.tensor_copy(out, in_), r, w)

    def mm(c0, n, lhsT, rhs, start, stop, r):
        op("T", lambda: PE.matmul(T.ps[:, c0:c0 + n], lhsT, rhs, start, stop), r, [("ps", c0, c0 + n)])

    def sel_g(out, in_, pat, cmp, base, cm, r, w):
        op("G", lambda: g.affine_select(out, in_, pat, cmp, 0.0, base, cm), r, w)

    def scaled(name, src, j, func=AF.Identity):
        act(T[name][:], T[src][:], func, [al(src), rc(j)], [al(name)], scale=col(j))

    def store(a, b):
        op("Y", lambda: g.sync.dma_start(T.yg[:, a:b], T.Pf[:, a:b]).then_inc(T.sem.stored, 16), [("Pf", a, b)], [], sem=("stored", 0))

    ld = spans(LOADS)
    for k, (a, b) in enumerate(ld):
        op("Y", lambda a=a, b=b, k=k: g.sync.dma_start(T.Pi[:, a:b], T.g0[:, a:b]).then_inc(T.sem["ld%d" % k], 16),
           [], [("Pi", a, b)], sem=("ld%d" % k, 16))
    for t in range(RO):
        ne = len(engines_of(srcs[t]))
        op("G", None, [], [("mi%d" % t, 0, 64)], sem=("ah%d" % t, ne))
        op("G", None, [], [("mi%d" % t, 64, 192)], sem=("ai%d" % t, ne))
        op("G", None, [], [al("mc%d" % t)], sem=("ac%d" % t, ne))

    op("V", lambda: V.memset(T.ones[:], 1.0), [], [al("ones")])
    op("V", lambda: V.memset(T.neg1[:], -1.0), [], [al("neg1")])
    op("G", lambda: g.iota(T.iotaT[0:6, :], [[1, NB]], -int(MID), NB, allow_small_or_imprecise_dtypes=True), [], [al("iotaT")])
    sel_g(T.ident[:], T.ones[:, 0:128], [[-1, 128]], ALU.is_equal, 0, 1, [al("ones")], [al("ident")])
    op("G", lambda: g.iota(T.tc[:, 0:1], [[1, 1]], 127, -1, allow_small_or_imprecise_dtypes=True), [], [("tc", 0, 1)])
    sel_g(T.G1[:], T.ones[:], [[-16, 9], [0, 16]], ALU.is_ge, 0, 1, [al("ones")], [al("G1")])
    sel_g(T.G2[:], T.G1[:], [[16, 9], [0, 16]], ALU.is_gt, 16, -1, [al("G1")], [al("G2")])
    sel_g(T.A0[:], T.G2[:], [[0, 9], [1, 16]], ALU.is_equal, -15, 0, [al("G2")], [al("A0")])
    sel_g(T.E16[:], T.neg1[:], [[-1, 16], [-16, 8], [0, 16]], ALU.is_equal, 0, 1, [al("neg1")], [al("E16")])
    act(T.codeT[0:6, :], T.iotaT[0:6, :], AF.Exp, [al("iotaT")], [al("codeT")], scale=CS)
    op("V", lambda: V.memset(T.huge[:], HUGE), [], [al("huge")])
    op("V", lambda: V.memset(col(14), 1.0), [], [rc(14)])
    vcopy(T.iotah[0:6, :], T.iotaT[0:6, :], [al("iotaT")], [al("iotah")])
    vcopy(T.identh[:], T.ident[:], [al("ident")], [al("identh")])
    for j in range(6):
        ts(T.negselh[0:6, 128 * j:128 * j + 128], T.neg1[0:6, 0:128], T.ident[0:6, j:j + 1], None, ALU.mult, None,
           [al("neg1"), al("ident")], [("negselh", 128 * j, 128 * j + 128)])

    def small_constants(part):
        if part == 1:
            vcopy(T.Gf[:], T.G2[:, 0:128], [al("G2")], [al("Gf")])
            ts(T.A0p[:], T.A0[:], 74.0, -200.0, ALU.mult, ALU.add, [al("A0")], [al("A0p")])
            ts(T.A0n[:], T.A0[:], BIG, -BIG, ALU.mult, ALU.add, [al("A0")], [al("A0n")])
            vcopy(T.negsel[0:6, :], T.negselh[0:6, :], [al("negselh")], [al("negsel")])
            return
        ts(T.wI[:], T.ident[:], WLT, None, ALU.mult, None, [al("ident")], [al("wI")])
        ts(T.nident[:], T.ident[:], -1.0, None, ALU.mult, None, [al("ident")], [al("nident")])
        ts(T.tc[:, 1:2], T.tc[:, 0:1], -1.0 / 128, -4096.0, ALU.mult, ALU.add, [("tc", 0, 1)], [("tc", 1, 2)])
        ts(T.st[:, 1:160:16], T.ones[:, 0:10], T.tc[:, 1:2], None, ALU.mult, None, [al("ones"), ("tc", 1, 2)],
           [rc(16 * j + 1) for j in range(10)])
        ts(T.tc[:, 2:3], T.tc[:, 1:2], 0.5, W / 2.0, ALU.mult, ALU.add, [("tc", 1, 2)], [("tc", 2, 3)])

    def place(sel, row, a, b, bank):
        j, o = a // NB, a % NB
        mm(bank * NB, b - a, T[sel][0:6, 128 * j:128 * j + 128], T[row][0:6, o:o + b - a], True, False, [al(sel), al(row)])

    def signs(c0, n, j, scale, jc, **kw):
        act(T.junk[:, jc:jc + n], T.ps[:, c0:c0 + n], AF.Sign, [("ps", c0, c0 + n)], [("junk", jc, jc + n), rc(j)],
            scale=scale, accum_out=col(j), **kw)

    def list_mm(sel, src, k0, k1, c0):
        for i in range(16):
            mm(c0, k1 - k0, T[sel][:, 15 - i:143 - i], T[src][:, 16 * k0 + i:16 * k1:16], i == 0, i == 15,
               [al(sel), (src, 16 * k0, 16 * k1)])

    def list_out(t, k0, k1, c0):
        n = k1 - k0
        li, lc = "li%d" % t, "lc%d" % t
        pp, rp = T.ps[:, c0:c0 + n], [("ps", c0, c0 + n)]
        if t == 0:
            ts(T[li][:, k0:k1], pp, MID, None, ALU.add, None, rp, [(li, k0, k1)])
            act(T[lc][:, k0:k1], pp, AF.Exp, rp, [(lc, k0, k1)], scale=CS)
        else:
            act(T.ly[:, k0:k1], pp, AF.Ln, rp, [("ly", k0, k1)])
            ts(T[li][:, k0:k1], T.ly[:, k0:k1], 1.0 / CS, MID + 0.25, ALU.mult, ALU.add, [("ly", k0, k1)], [(li, k0, k1)])
            act(T[lc][:, k0:k1], pp, AF.Identity, rp, [(lc, k0, k1)])

    def send(t, src, dst, sem, a, b):
        rid, pid = topo.addr(dests[t])[0:2]
        op("G", lambda: g.remote_dma(T[dst][:, a:b], T[src][:, a:b], T.sem[sem], T.sem.sent, pid, rid, my_mask),
           [(src, a, b)], [], sem=("sent", 0))

    bank = [0]

    def next_bank():
        bank[0] = (bank[0] + 1) % 6
        return bank[0]

    def encode_mm(a, b):
        j = next_bank()
        mm(j * NB, b - a, T.identh[:], T.Ph[:, a:b], True, True, [al("identh"), ("Ph", a, b)])
        return j

    def encode(a, b, j):
        act(T.P[:, a:b], T.ps[:, j * NB:j * NB + b - a], AF.Exp, [("ps", j * NB, j * NB + b - a)], [("P", a, b)], scale=CS)

    for k, (a, b) in enumerate(ld):
        ts(T.Ph[:, a:b], T.Pi[:, a:b], -MID, None, ALU.add, None, [("Pi", a, b)], [("Ph", a, b)])
        if k < 2:
            small_constants(k)
        j = next_bank()
        place("negselh", "iotah", a, b, j)
        mm(j * NB, b - a, T.identh[:], T.Ph[:, a:b], False, True, [al("identh"), ("Ph", a, b)])
        signs(j * NB, b - a, 2 + k, -1.0, a, bias=0.5)
        if k < EARLY:
            encode(a, b, encode_mm(a, b))
    late = [(a, b, encode_mm(a, b)) for a, b in ld[EARLY:]]
    op("V", lambda: V.tensor_reduce(col(16), T.st[:, 1:2 + len(ld)], AxisListType.X, ALU.add, negate=True), [rc(1, 1 + len(ld))], [rc(16)])
    ts(T.R[:], T.ident[:], col(16), None, ALU.mult, None, [al("ident"), rc(16)], [al("R")])
    mm(6 * NB, 128, T.Gf[:], T.R[:], True, True, [al("Gf"), al("R")])
    op("V", lambda: V.tensor_reduce(col(13), T.ps[:, 6 * NB:6 * NB + 128], AxisListType.X, ALU.max), [("ps", 6 * NB, 7 * NB)], [rc(13)])
    ts(T.Ah[:], T.A0n[:], col(16), col(13), ALU.add, ALU.is_ge, [al("A0n"), rc(16), rc(13)], [al("Ah")])
    for a, b, j in late:
        encode(a, b, j)

    sg, wsig = 14, "wI"
    for t in range(RO):
        k0, k1, k2 = 16 * (1 + 2 * t), 16 * (2 + 2 * t), 16 * (3 + 2 * t)
        li, lc, mi, mc = "li%d" % t, "lc%d" % t, "mi%d" % t, "mc%d" % t
        last = t == RO - 1
        own = OWN if t == 0 else 192
        lsel, lsrc = ("Ah", "Ph") if t == 0 else ("A", "P")
        list_mm(lsel, lsrc, 0, 64, 6 * NB)
        list_mm(lsel, lsrc, 64, 128, NB - 64)
        list_mm(lsel, lsrc, 128, 192, NB)
        list_out(t, 0, 64, 6 * NB)
        send(t, li, mi, "ah%d" % t, 0, 64)
        ch = spans(CNT0)

        def gather(a, b, on_s, li=li):
            win = lambda: T.P[:, 0:W].indirect(T[li][:, a // 16:b // 16])
            r, w = [al("P"), (li, a // 16, b // 16)], [("H0", a, b)]
            if on_s:
                op("S", lambda: S.activation(T.H0[:, a:b], win(), AF.Identity), r, w)
            else:
                op("V", lambda: V.tensor_copy(T.H0[:, a:b], win()), r, w)

        gs = [(a, b, who == "S") for (a, b), (n, who) in zip(spans([m[0] for m in GATH]), GATH)]
        gather(*gs[0])
        gather(*gs[1])
        list_out(t, 64, 192, NB - 64)
        send(t, li, mi, "ai%d" % t, 64, own)
        send(t, lc, mc, "ac%d" % t, 0, 192)
        for m in gs[2:]:
            gather(*m)
        for k, (a, b) in enumerate(ch):
            j = (k + 2) % 8
            cut = min(b, (a // NB + 1) * NB)
            for a2, b2 in ((a, cut), (cut, b)):
                if b2 > a2:
                    jj, o = a2 // NB, a2 % NB
                    c0 = j * NB + a2 - a
                    mm(c0, b2 - a2, T.negsel[0:6, 128 * jj:128 * jj + 128], T.codeT[0:6, o:o + b2 - a2], True, False, [al("negsel"), al("codeT")])
                    mm(c0, b2 - a2, T[wsig][:], T.H0[:, a2:b2], False, True, [al(wsig), ("H0", a2, b2)])
            signs(j * NB, b - a, k0 + 2 + k, -1.0 if k < len(ch) - 1 else 1.0, a)
        kk, pp = k0 + 10, k0 + 1 + len(ch)
        op("V", lambda kk=kk, k0=k0, pp=pp: V.tensor_reduce(col(kk), T.st[:, k0:pp], AxisListType.X, ALU.add), [rc(k0, pp - k0)], [rc(kk)])
        ca, cn = k0 + 12, k0 + 13
        ts(col(ca), col(pp), col(kk), col(sg), ALU.is_gt, ALU.mult, [rc(pp), rc(kk), rc(sg)], [rc(ca)])
        ts(col(cn), col(pp), col(kk), col(sg), ALU.is_le, ALU.mult, [rc(pp), rc(kk), rc(sg)], [rc(cn)])
        scaled("Wa", "ident", ca)
        scaled("Wna", "ident", cn)
        ts(T.tA[:], T.H0[:, 0:FIRST], col(ca), None, ALU.mult, None, [("H0", 0, FIRST), rc(ca)], [al("tA")])
        ts(T.tB[:], T.P[:, 0:FIRST], col(cn), None, ALU.mult, None, [("P", 0, FIRST), rc(cn)], [al("tB")])
        ts(col(k0 + 11), col(pp), col(kk), 0.0, ALU.subtract, ALU.max, [rc(kk), rc(pp)], [rc(k0 + 11)])
        op("V", lambda mi=mi: V.tensor_tensor(T.H1[:, 0:W].indirect(T[mi][:, 0:FIRST // 16]), T.tA[:], T.tB[:], ALU.add),
           [al("tA"), al("tB"), (mi, 0, FIRST // 16)], [al("H1")])
        sel = spans(SEL, FIRST)
        for k, (a, b) in enumerate(sel[:2] + [(0, FIRST)] + sel[2:]):
            c0 = (6, 7, 4)[k % 3] * NB
            mm(c0, b - a, T.Wa[:], T.H0[:, a:b], True, False, [al("Wa"), ("H0", a, b)])
            mm(c0, b - a, T.Wna[:], T.P[:, a:b], False, True, [al("Wna"), ("P", a, b)])
            act(T.P1[:, a:b], T.ps[:, c0:c0 + b - a], AF.Identity, [("ps", c0, c0 + b - a)], [("P1", a, b)])
        act(col(k1), col(k0 + 11), AF.Identity, [rc(k0), rc(k0 + 11)], [rc(k1)], bias=col(k0))
        if own < 192:
            act(T.my[:], T[mc][:, own:192], AF.Ln, [al(mc)], [al("my")])
        for a, b in spans(SCAT, FIRST):
            if a // 16 >= own:
                if a // 16 == own:
                    ts(T.mx[:], T.my[:], 1.0 / CS, MID + 0.25, ALU.mult, ALU.add, [al("my")], [al("mx")])
                off, ro = T.mx[:, a // 16 - own:b // 16 - own], al("mx")
            else:
                off, ro = T[mi][:, a // 16:b // 16], (mi, a // 16, b // 16)
            op("V", lambda a=a, b=b, off=off: V.tensor_copy(T.H1[:, 0:W].indirect(off), T.P1[:, a:b]), [("P1", a, b), ro], [al("H1")])
        for c in range(3):
            for i in range(16):
                c0 = 1024 * c + 64 * i
                mm(c0, 64, T.wI[:], T.P1[:, 1024 * c + i:1024 * (c + 1):16], True, False, [al("wI"), ("P1", 1024 * c, 1024 * (c + 1))])
                mm(c0, 64, T.E16[:, 128 * i:128 * i + 128], T[mc][:, 64 * c:64 * c + 64], False, True, [al("E16"), al(mc)])
                if c == 0 and i % 8 == 7:
                    signs(NB * (i // 8), NB, k1 + 2 + i // 8, -1.0, NB * (i // 8))
            if c > 0:
                signs(1024 * c, 1024, k1 + 3 + c, -1.0, 1024 * c)
        mix = OUT if last else MIX
        mix = [(a, b, j * NB, who == "V" and not last) for (a, b), (n, j, who) in zip(spans([m[0] for m in mix]), mix)]
        for a, b, c0, direct in mix:
            if direct:
                mm(c0, b - a, T.nident[:], T.P1[:, a:b], True, False, [al("nident"), ("P1", a, b)])
        cd, cr, cm, cs = k1 + 10, k1 + 11, k1 + 12, k1 + 14
        act(T.junkf[:, 0:6], T.st[:, k1:k1 + 6], AF.Identity, [rc(k1, 6)], [al("junkf"), rc(cd)], accum_out=col(cd))
        act(col(cm), col(cd), AF.Relu, [rc(cd)], [rc(cm)], bias=1.0)
        act(col(cr), col(cd), AF.Relu, [rc(cd)], [rc(cr)], scale=-1.0)
        scaled("Wnb", "ident" if last else "nident", cm, AF.Sign)
        scaled("Wb", "ident", cr, AF.Sign)
        act(col(k2), col(cr), AF.Identity, [rc(cr), rc(k1)], [rc(k2)], bias=col(k1))
        if not last:
            scaled("R", "ident", k2)
        for a, b, c0, direct in mix:
            if not direct:
                mm(c0, b - a, T.Wnb[:], T.P1[:, a:b], True, False, [al("Wnb"), ("P1", a, b)])
        for a, b, c0, direct in mix:
            if direct:
                mm(c0, b - a, T.Wb[:], T.huge[:, 0:b - a], False, True, [al("Wb"), al("huge")])
        if not last:
            mm(6 * NB, 128, T.Gf[:], T.R[:], True, True, [al("Gf"), al("R")])
            act(col(cs), col(cr), AF.Sign, [rc(cr)], [rc(cs)], bias=-1.0)
            act(T.junk2[:], T.ps[:, 6 * NB:6 * NB + 128], AF.Sign, [("ps", 6 * NB, 7 * NB), rc(k2)], [al("junk2"), rc(k1 + 13)],
                scale=-1.0, bias=col(k2), accum_out=col(k1 + 13))
            scaled("Ws", "wI", cs)
            act(T.A1[:], T.A0p[:], AF.Relu, [al("A0p"), rc(k1 + 13)], [al("A1")], bias=col(k1 + 13))
            scaled("A", "A1", cs)
            sg, wsig = cs, "Ws"
        else:
            act(T.yec[:], col(k2), AF.Identity, [rc(k2), ("tc", 2, 3)], [al("yec")], scale=0.5, bias=T.tc[:, 2:3])
            op("Y", lambda: g.sync.dma_start(T.ye[:], T.yec[:]).then_inc(T.sem.stored, 16), [al("yec")], [], sem=("stored", 0))
        for a, b, c0, direct in mix:
            pc, rp = T.ps[:, c0:c0 + b - a], ("ps", c0, c0 + b - a)
            if direct:
                op("V", lambda a=a, b=b, pc=pc: V.tensor_tensor(T.P[:, a:b], T.H1[:, a:b], pc, ALU.min), [("H1", a, b), rp], [("P", a, b)])
            else:
                mm(c0, b - a, T.Wb[:], T.H1[:, a:b], False, True, [al("Wb"), ("H1", a, b)])
                if not last:
                    act(T.P[:, a:b], pc, AF.Identity, [rp], [("P", a, b)])

    held = []
    for (a, b), (n, j, who) in zip(spans([m[0] for m in OUT]), OUT):
        pf, rw = T.Pf[:, a:b], [("Pf", a, b)]
        act(pf, T.ps[:, j * NB:j * NB + n], AF.Ln, [("ps", j * NB, j * NB + n)], rw)
        ts(pf, pf, 1.0 / CS, MAGIC + MID, ALU.mult, ALU.add, rw, rw)
        if who == "V":
            ts(pf, pf, -MAGIC, None, ALU.add, None, rw, rw)
            store(a, b)
        else:
            held.append((a, b))
    for a2, b2 in held:
        act(T.Pf[:, a2:b2], T.Pf[:, a2:b2], AF.Identity, [("Pf", a2, b2)], [("Pf", a2, b2)], bias=-MAGIC)
        store(a2, b2)

    emit(g, T, ops)
    g.wait_ge(T.sem.sent, 3 * RO * len(my_eng))
    g.sync.wait_ge(T.sem.stored, 16 * (1 + len(OUT)))
